import numpy as np
import ml_dtypes


def mxq(x, axis, fmt="e4m3"):
    dtype, down = {"e4m3": (ml_dtypes.float8_e4m3fn, 7), "e5m2": (ml_dtypes.float8_e5m2, 14)}[fmt]
    v = np.moveaxis(np.asarray(x, np.float32).astype(ml_dtypes.bfloat16).astype(np.float64), axis, -1)
    blocks = v.reshape(v.shape[:-1] + (-1, 32))
    amax = np.abs(blocks).max(-1, keepdims=True)
    byte = np.maximum(np.where(amax > 0, np.frexp(amax)[1] - 1 + 127, 0) - down, 1)
    scale = np.exp2(byte - 127.0)
    codes = (blocks / scale).astype(np.float32).astype(dtype).astype(np.float64)
    return np.moveaxis((codes * scale).reshape(v.shape), -1, axis)


WIDE = False


def mx_kscale(k):
    if not WIDE:
        return np.ones(k)
    levels = np.array([10, -10, 5, -5, 0])
    if k % 512:
        return np.exp2(np.random.permutation(np.resize(levels, k // 32))).repeat(32)
    a = np.empty((k // 512, 16))
    for p in range(k // 512):
        a[p, :8] = np.random.permutation(np.resize(levels, 8))
        for g in range(8):
            far = levels[np.abs(levels - a[p, g]) >= 10]
            a[p, g + 8] = far[np.random.randint(len(far))]
    return np.exp2(a.ravel()).repeat(32)


def f64(x):
    return np.asarray(x).astype(np.float64)


def striped(idx):
    return np.tile(np.asarray(idx).reshape(-1, 16).T, (8, 1)).astype(np.uint16)


def unstriped(offs):
    return offs[:16].T.reshape(-1).astype(np.int64)


E2M1 = np.array([0.0, 0.5, 1.0, 1.5, 2.0, 3.0, 4.0, 6.0, -0.0, -0.5, -1.0, -1.5, -2.0, -3.0, -4.0, -6.0])


def pack_weight(w, fmt):
    k, n = w.shape
    w = f64(np.asarray(w, np.float32).astype(ml_dtypes.bfloat16)).reshape(k // 32, 32, n)
    amax = np.abs(w).max(1)
    if fmt == "e4m3":
        byte = np.frexp(amax)[1] - 1 + 127 - 7
    else:
        mant, ex = np.frexp(amax / 6.0)
        byte = np.where(mant > 0.5, ex, ex - 1) + 127
    byte = np.clip(np.where(amax > 0, byte, 1), 1, 254)
    scaled = (w * np.exp2(127.0 - byte)[:, None, :]).reshape(k, n).astype(np.float32)
    by_word = np.ascontiguousarray(scaled.reshape(k // 512, 128, 4, n).transpose(0, 1, 3, 2))
    if fmt == "e4m3":
        words = by_word.astype(ml_dtypes.float8_e4m3fn).view(np.uint8)
    else:
        c = by_word.astype(ml_dtypes.float4_e2m1fn).view(np.uint8) & 0xF
        words = (c[..., 0::2] | (c[..., 1::2] << 4)).reshape(k // 512, 128, 2 * n)
    return np.ascontiguousarray(words), np.ascontiguousarray(byte.astype(np.uint8).reshape(k // 512, 16, n))


def unpack_weight(words, scales, fmt):
    g, _, n = scales.shape
    words = np.ascontiguousarray(words).reshape(g, 128, n, -1)
    if fmt == "e4m3":
        vals = words.view(ml_dtypes.float8_e4m3fn).astype(np.float64)
    else:
        nib = np.empty((g, 128, n, 4), np.uint8)
        nib[..., 0::2] = words & 0xF
        nib[..., 1::2] = words >> 4
        vals = E2M1[nib]
    vals = vals * np.repeat(np.exp2(scales.astype(np.float64) - 127.0), 8, axis=1)[..., None]
    return vals.transpose(0, 1, 3, 2).reshape(g * 512, n)


D, E, T, I, Q = 512, 512, 1024, 512, 128


def setup_inputs():
    n = np.random.standard_normal
    idx = np.random.permutation(T)[:I]
    idx2 = np.random.permutation(T)[:I]
    idx3 = np.random.permutation(T)[:I]
    fd = mx_kscale(D)
    fe = mx_kscale(E)
    fi = mx_kscale(I)
    keysp = pack_weight(n((D, T)) / fd[:, None], "e4m3")
    valsp = pack_weight(n((E, T)) / fe[:, None], "e4m3")
    return {
        "query": (n((D, Q)) * 0.5 / np.sqrt(D) * fd[:, None]).astype(np.float32),
        "keys_words": keysp[0],
        "keys_scales": keysp[1],
        "gout": (n((E, Q)) * 1 / np.sqrt(E) * fe[:, None]).astype(np.float32),
        "vals_words": valsp[0],
        "vals_scales": valsp[1],
        "lse": (np.random.uniform(6.9, 7.2, (Q, 1))).astype(np.float32),
        "delta": (np.random.uniform(-0.3, 0.3, (Q, 1))).astype(np.float32),
        "fs": (np.random.uniform(128.0, 512.0, (1, I)) * fi).astype(np.float32),
        "keyrows": (n((D, T))).astype(np.float32),
        "ksc": (np.random.uniform(0.5, 2.0, (I, 1)) / fi[:, None]).astype(np.float32),
        "res": (n((Q, D)) * 4.0).astype(np.float32),
        "offs": striped(idx),
        "offs2": striped(idx2),
        "offs3": striped(idx3),
    }


def reference(query, keys_words, keys_scales, gout, vals_words, vals_scales, lse, delta, fs, keyrows, ksc, res, offs, offs2, offs3):
    idx = unstriped(offs)
    idx2 = unstriped(offs2)
    idx3 = unstriped(offs3)
    keysu = unpack_weight(keys_words, keys_scales, "e4m3")
    valsu = unpack_weight(vals_words, vals_scales, "e4m3")
    queryq = mxq(f64(query), 0, "e4m3")
    keysidxg = keysu[:, idx]
    a = queryq.T @ keysidxg
    keysidx2g = keysu[:, idx2]
    b = queryq.T @ keysidx2g
    pa = np.exp(a - f64(lse))
    pb = np.exp(b - f64(lse))
    goutq = mxq(f64(gout), 0, "e4m3")
    valsidx3g = valsu[:, idx3]
    dp = goutq.T @ valsidx3g
    dd = (dp - f64(delta)) * f64(fs)
    da = pa * dd
    db = pb * dd
    ta = da.T
    tb = db.T
    ka = f64(keyrows)[:, idx].T
    kb = f64(keyrows)[:, idx2].T
    k1 = ka * f64(ksc)
    k2 = kb * f64(ksc)
    taq = mxq(ta, 0, "e4m3")
    k1q = mxq(k1, 0, "e4m3")
    tbq = mxq(tb, 0, "e4m3")
    k2q = mxq(k2, 0, "e4m3")
    gq = taq.T @ k1q + tbq.T @ k2q
    y = gq + f64(res)
    return y

@@ -1,0 +1,180 @@
+from contextlib import ExitStack
+
+import concourse.mybir as mybir
+from concourse.masks import make_identity
+
+D, E, T, I, Q = 512, 512, 1024, 512, 128
+FLOPS = 2 * Q * I * (2 * D + E) + 2 * 2 * Q * I * D
+
+F32 = mybir.dt.float32
+BF16 = mybir.dt.bfloat16
+I32 = mybir.dt.int32
+U32 = mybir.dt.uint32
+U16 = mybir.dt.uint16
+U8 = mybir.dt.uint8
+FP8X4 = mybir.dt.float8_e4m3fn_x4
+ACT = mybir.ActivationFunctionType
+ALU = mybir.AluOpType
+
+P = 128
+PACK = 4
+PLANES = D // P
+
+
+def tile_attend_gsynonyms_kernel(tc, query, keys_words, keys_scales, gout, vals_words, vals_scales, lse, delta, fs,
+                                  keyrows, ksc, res, offs, offs2, offs3, out):
+    nc = tc.nc
+    with ExitStack() as ctx:
+        keep = ctx.enter_context(tc.tile_pool(name="keep", bufs=1))
+        psum = ctx.enter_context(tc.psum_pool(name="psum", bufs=1))
+
+        def load_list(name, src):
+            tile = keep.tile([P, I // 16], U16, name=name)
+            nc.sync.dma_start(tile[:], src)
+            return tile
+
+        def load_scales(name, src):
+            tile = keep.tile([P, T], U8, name=name)
+            nc.gpsimd.memset(tile[:].bitcast(I32), 0)
+            rows = src[0].bitcast(I32)
+            for quad in range(4):
+                nc.sync.dma_start(tile[32 * quad : 32 * quad + 4, :].bitcast(I32), rows[4 * quad : 4 * quad + 4, :])
+            return tile
+
+        def load_words(name, src):
+            tile = keep.tile([P, T], U32, name=name)
+            nc.sync.dma_start(tile[:].bitcast(I32), src[0].rearrange("p t b -> p (t b)").bitcast(I32))
+            return tile
+
+        def load(name, shape, src):
+            tile = keep.tile(shape, F32, name=name)
+            nc.sync.dma_start(tile[:], src)
+            return tile
+
+        list_a = load_list("list_a", offs)
+        key_scale_pool = load_scales("key_scale_pool", keys_scales)
+        list_b = load_list("list_b", offs2)
+        val_word_pool = load_words("val_word_pool", vals_words)
+        list_v = load_list("list_v", offs3)
+        val_scale_pool = load_scales("val_scale_pool", vals_scales)
+        key_word_pool = load_words("key_word_pool", keys_words)
+        gout_raw = load("gout_raw", [P, PACK, Q], gout.rearrange("(p r) q -> p r q", r=PACK))
+        query_raw = load("query_raw", [P, PACK, Q], query.rearrange("(p r) q -> p r q", r=PACK))
+        ksc_cols = load("ksc_cols", [P, PACK], ksc.rearrange("(s r) o -> s (r o)", r=PACK))
+        key_planes = [load("key_plane0", [P, T], keyrows[0:P, :])]
+        delta_col = load("delta_col", [P, 1], delta)
+        lse_col = load("lse_col", [P, 1], lse)
+        fs_cols = load("fs_cols", [P, PACK], fs.rearrange("o (s r) -> s (o r)", r=PACK))
+        for j in range(1, PLANES):
+            key_planes.append(load("key_plane%d" % j, [P, T], keyrows[j * P : (j + 1) * P, :]))
+        res_rows = load("res_rows", [P, D], res)
+
+        ident = keep.tile([P, P], F32, name="ident")
+        make_identity(nc, ident[:])
+
+        def gather(name, pool_tile, slots, dtype):
+            tile = keep.tile([P, I], dtype, name=name, align_bytes=64)
+            nc.vector.tensor_copy(tile[:], pool_tile[:].indirect(slots[:]))
+            return tile
+
+        def quantize(name, grouped):
+            width = grouped.shape[1]
+            codes = keep.tile([P, width], U32, name=name + "_codes", align_bytes=64)
+            scales = keep.tile([P, width], U8, name=name + "_scales", align_bytes=64)
+            nc.vector.quantize_mx(codes[:].bitcast(FP8X4), scales[:], grouped[:].rearrange("p c r -> p (c r)"))
+            return codes, scales
+
+        def product(acc, stationary, moving, start, stop):
+            nc.tensor.matmul_mx(acc, lhsT=stationary[0][:].bitcast(FP8X4), lhsT_scale=stationary[1][:],
+                                rhs=moving[0][:].bitcast(FP8X4), rhs_scale=moving[1][:], start=start, stop=stop)
+
+        def group_rows(name, raw):
+            grouped = keep.tile([P, Q, PACK], BF16, name=name, align_bytes=64)
+            nc.scalar.copy(grouped[:], raw[:].rearrange("p r q -> p q r"))
+            return grouped
+
+        def turn(name, bank, by_place):
+            turned = psum.tile([P, PACK, Q], F32, name=name, tag=bank)
+            for r in range(PACK):
+                nc.tensor.transpose(turned[:, r, :], by_place[:, r, :], ident[:])
+            return turned
+
+        a_scales = gather("a_scales", key_scale_pool, list_a, U8)
+        b_scales = gather("b_scales", key_scale_pool, list_b, U8)
+        v_words = gather("v_words", val_word_pool, list_v, U32)
+        v_scales = gather("v_scales", val_scale_pool, list_v, U8)
+        gout_mx = quantize("gout", group_rows("gout_grouped", gout_raw))
+        a_words = gather("a_words", key_word_pool, list_a, U32)
+        query_mx = quantize("query", group_rows("query_grouped", query_raw))
+        b_words = gather("b_words", key_word_pool, list_b, U32)
+
+        ksc_turned = psum.tile([P, PACK, P], F32, name="ksc_turned", tag="bank_e")
+        for r in range(PACK):
+            nc.tensor.transpose(ksc_turned[:, r, :], ksc_cols[:, r : r + 1].to_broadcast([P, P]), ident[:])
+        ksc_row = keep.tile([P, I], F32, name="ksc_row")
+        nc.scalar.copy(ksc_row[:].rearrange("p (s r) -> p s r", r=PACK), ksc_turned[:].rearrange("p r s -> p s r"))
+
+        neg_delta = keep.tile([P, 1], F32, name="neg_delta")
+        nc.scalar.mul(neg_delta[:], delta_col[:], -1.0)
+        neg_lse = keep.tile([P, 1], F32, name="neg_lse")
+        nc.scalar.mul(neg_lse[:], lse_col[:], -1.0)
+
+        def scores(name, bank, rows_mx, words, scales, func, bias):
+            acc = psum.tile([P, I], F32, name=name + "_acc", tag=bank)
+            product(acc[:], rows_mx, (words, scales), True, True)
+            by_place = keep.tile([P, PACK, P], F32, name=name + "_by_place")
+            nc.scalar.activation(by_place[:], acc[:].rearrange("q (s r) -> q r s", r=PACK), func, bias=bias[:])
+            return by_place
+
+        centred = scores("dp", "bank_v", gout_mx, v_words, v_scales, ACT.Identity, neg_delta)
+        centred_t = turn("centred_t", "bank_e", centred)
+        dd_by_place = keep.tile([P, PACK, Q], F32, name="dd_by_place")
+        for r in range(PACK):
+            nc.scalar.activation(dd_by_place[:, r, :], centred_t[:, r, :], ACT.Copy, scale=fs_cols[:, r : r + 1])
+        dd_grouped = keep.tile([P, Q, PACK], F32, name="dd_grouped")
+        nc.scalar.copy(dd_grouped[:], dd_by_place[:].rearrange("s r q -> s q r"))
+
+        weights_t = []
+        for name, words, scales in (("a", a_words, a_scales), ("b", b_words, b_scales)):
+            weight = scores(name, "bank_" + name, query_mx, words, scales, ACT.Exp, neg_lse)
+            weights_t.append(turn(name + "_weight_t", "bank_" + name, weight))
+
+        def gather_keys(j, name, slots):
+            scaled = keep.tile([P, I], F32, name="scaled_%s%d" % (name, j))
+            nc.vector.tensor_tensor(scaled[:], key_planes[j][:].indirect(slots[:]), ksc_row[:], ALU.mult)
+            paired = keep.tile([P, 2, P, 2], BF16, name="paired_%s%d" % (name, j))
+            nc.scalar.copy(paired[:], scaled[:].rearrange("d (s u e) -> d u s e", u=2, e=2))
+            words = paired[:].rearrange("d u s e -> d (u s e)").bitcast(F32)
+            turned = psum.tile([P, 2, P], F32, name="keys_turned", bufs=2)
+            for u in range(2):
+                nc.tensor.transpose(turned[:, u, :], words[:, u * P : (u + 1) * P], ident[:])
+            grouped = keep.tile([P, P, PACK], BF16, name="grouped_%s%d" % (name, j), align_bytes=64)
+            nc.scalar.copy(grouped[:].rearrange("s d r -> s (d r)").bitcast(F32).rearrange("s (d u) -> s d u", u=2),
+                           turned[:].rearrange("s u d -> s d u"))
+            return grouped
+
+        def weight_grad(name, weight_t):
+            grouped = keep.tile([P, Q, PACK], BF16, name="grad_" + name, align_bytes=64)
+            nc.vector.tensor_tensor(grouped[:], weight_t[:].rearrange("s r q -> s q r"), dd_grouped[:], ALU.mult)
+            return grouped
+
+        grouped_keys = {}
+        grouped_keys[0] = (gather_keys(0, "a", list_a), gather_keys(0, "b", list_b))
+        grads = [weight_grad("a", weights_t[0]), weight_grad("b", weights_t[1])]
+        grouped_keys[1] = (gather_keys(1, "a", list_a), gather_keys(1, "b", list_b))
+        grads_mx = [quantize("grad_a", grads[0]), quantize("grad_b", grads[1])]
+
+        def finish(j):
+            acc = psum.tile([P, P], F32, name="out_acc", bufs=2)
+            for side, name in enumerate("ab"):
+                keys_mx = quantize("keys_%s%d" % (name, j), grouped_keys[j][side])
+                product(acc[:], grads_mx[side], keys_mx, side == 0, side == 1)
+            cols = slice(j * P, (j + 1) * P)
+            result = keep.tile([P, P], F32, name="result%d" % j)
+            nc.vector.tensor_tensor(result[:], acc[:], res_rows[:, cols], ALU.add)
+            nc.sync.dma_start(out[:, cols], result[:])
+
+        for j in range(2, PLANES):
+            grouped_keys[j] = (gather_keys(j, "a", list_a), gather_keys(j, "b", list_b))
+        for j in range(PLANES):
+            finish(j)

@@ -35,10 +35,11 @@ def tile_attend_gsynonyms_kernel(tc, query, keys_words, keys_scales, gout, vals_
 
         def load_scales(name, src):
             tile = keep.tile([P, T], U8, name=name)
-            nc.gpsimd.memset(tile[:].bitcast(I32), 0)
             rows = src[0].bitcast(I32)
             for quad in range(4):
-                nc.sync.dma_start(tile[32 * quad : 32 * quad + 4, :].bitcast(I32), rows[4 * quad : 4 * quad + 4, :])
+                queue = nc.sync if quad < 2 else nc.scalar
+                queue.dma_start(tile[32 * quad : 32 * quad + 32, :].bitcast(I32),
+                                  rows[4 * quad : 4 * quad + 4, :].unsqueeze(0).to_broadcast([8, 4, T // 4]))
             return tile
 
         def load_words(name, src):
@@ -77,9 +78,9 @@ def tile_attend_gsynonyms_kernel(tc, query, keys_words, keys_scales, gout, vals_
             nc.vector.tensor_copy(tile[:], pool_tile[:].indirect(slots[:]))
             return tile
 
-        def quantize(name, grouped):
+        def quantize(name, grouped, tag=""):
             width = grouped.shape[1]
-            codes = keep.tile([P, width], U32, name=name + "_codes", align_bytes=64)
+            codes = keep.tile([P, width], U32, name=name + "_codes", tag=tag, align_bytes=64)
             scales = keep.tile([P, width], U8, name=name + "_scales", align_bytes=64)
             nc.vector.quantize_mx(codes[:].bitcast(FP8X4), scales[:], grouped[:].rearrange("p c r -> p (c r)"))
             return codes, scales
@@ -139,42 +140,79 @@ def tile_attend_gsynonyms_kernel(tc, query, keys_words, keys_scales, gout, vals_
             weight = scores(name, "bank_" + name, query_mx, words, scales, ACT.Exp, neg_lse)
             weights_t.append(turn(name + "_weight_t", "bank_" + name, weight))
 
-        def gather_keys(j, name, slots):
-            scaled = keep.tile([P, I], F32, name="scaled_%s%d" % (name, j))
-            nc.vector.tensor_tensor(scaled[:], key_planes[j][:].indirect(slots[:]), ksc_row[:], ALU.mult)
-            paired = keep.tile([P, 2, P, 2], BF16, name="paired_%s%d" % (name, j))
-            nc.scalar.copy(paired[:], scaled[:].rearrange("d (s u e) -> d u s e", u=2, e=2))
+        def gather_keys(j, name, slots, cuts=(0, I)):
+            paired = keep.tile([P, 2, P, 2], BF16, name="paired", tag="paired_%s%d" % (name, j), align_bytes=64)
+            for piece in range(len(cuts) - 1):
+                lo, hi = cuts[piece], cuts[piece + 1]
+                scaled = keep.tile([P, hi - lo], F32, name="scaled", tag="scaled_%s%d_%d" % (name, j, piece), align_bytes=64)
+                nc.vector.tensor_tensor(scaled[:], key_planes[j][:].indirect(slots[:, lo // 16 : hi // 16]),
+                                        ksc_row[:, lo:hi], ALU.mult)
+                nc.scalar.copy(paired[:, :, lo // PACK : hi // PACK, :],
+                               scaled[:].rearrange("d (s u e) -> d u s e", u=2, e=2))
+            return paired
+
+        def turn_keys(paired, grouped):
             words = paired[:].rearrange("d u s e -> d (u s e)").bitcast(F32)
-            turned = psum.tile([P, 2, P], F32, name="keys_turned", bufs=2)
+            turned = psum.tile([P, 2, P], F32, name="keys_turned", bufs=4)
             for u in range(2):
                 nc.tensor.transpose(turned[:, u, :], words[:, u * P : (u + 1) * P], ident[:])
-            grouped = keep.tile([P, P, PACK], BF16, name="grouped_%s%d" % (name, j), align_bytes=64)
-            nc.scalar.copy(grouped[:].rearrange("s d r -> s (d r)").bitcast(F32).rearrange("s (d u) -> s d u", u=2),
+            nc.scalar.copy(grouped.rearrange("s d r -> s (d r)").bitcast(F32).rearrange("s (d u) -> s d u", u=2),
                            turned[:].rearrange("s u d -> s d u"))
-            return grouped
 
-        def weight_grad(name, weight_t):
-            grouped = keep.tile([P, Q, PACK], BF16, name="grad_" + name, align_bytes=64)
-            nc.vector.tensor_tensor(grouped[:], weight_t[:].rearrange("s r q -> s q r"), dd_grouped[:], ALU.mult)
-            return grouped
+        def cut(mx, lo, hi):
+            return mx[0][:, lo:hi], mx[1][:, lo:hi]
 
-        grouped_keys = {}
-        grouped_keys[0] = (gather_keys(0, "a", list_a), gather_keys(0, "b", list_b))
-        grads = [weight_grad("a", weights_t[0]), weight_grad("b", weights_t[1])]
-        grouped_keys[1] = (gather_keys(1, "a", list_a), gather_keys(1, "b", list_b))
-        grads_mx = [quantize("grad_a", grads[0]), quantize("grad_b", grads[1])]
+        def multiply(acc, keys_a, keys_b):
+            product(acc, cut(grads_mx, 0, Q), keys_a, True, False)
+            product(acc, cut(grads_mx, Q, 2 * Q), keys_b, False, True)
 
-        def finish(j):
-            acc = psum.tile([P, P], F32, name="out_acc", bufs=2)
-            for side, name in enumerate("ab"):
-                keys_mx = quantize("keys_%s%d" % (name, j), grouped_keys[j][side])
-                product(acc[:], grads_mx[side], keys_mx, side == 0, side == 1)
-            cols = slice(j * P, (j + 1) * P)
-            result = keep.tile([P, P], F32, name="result%d" % j)
-            nc.vector.tensor_tensor(result[:], acc[:], res_rows[:, cols], ALU.add)
-            nc.sync.dma_start(out[:, cols], result[:])
+        def finish(acc, lo, hi, tag=""):
+            result = keep.tile([P, hi - lo], F32, name="result%d" % lo, tag=tag, align_bytes=64)
+            nc.vector.tensor_tensor(result[:], acc[:], res_rows[:, lo:hi], ALU.add)
+            nc.sync.dma_start(out[:, lo:hi], result[:])
 
-        for j in range(2, PLANES):
-            grouped_keys[j] = (gather_keys(j, "a", list_a), gather_keys(j, "b", list_b))
-        for j in range(PLANES):
-            finish(j)
+        def grouped_tile(name, width, tag=""):
+            return keep.tile([P, width, PACK], BF16, name=name, tag=tag or name, align_bytes=64)
+
+        keys0 = grouped_tile("keys0", 2 * P)
+        keys1 = grouped_tile("keys1", 2 * P)
+        keys2 = grouped_tile("keys2", 2 * P)
+        keys3_b = grouped_tile("keys3_b", P)
+
+        paired_a = gather_keys(0, "a", list_a)
+        paired_b = gather_keys(0, "b", list_b)
+        turn_keys(paired_a, keys0[:, 0:P, :])
+        paired_a = gather_keys(1, "a", list_a)
+        turn_keys(paired_b, keys0[:, P : 2 * P, :])
+        paired_b = gather_keys(1, "b", list_b)
+        turn_keys(paired_a, keys1[:, 0:P, :])
+        grads = grouped_tile("grads", 2 * Q)
+        for side in range(2):
+            nc.vector.tensor_tensor(grads[:, side * Q : (side + 1) * Q, :], weights_t[side][:].rearrange("s r q -> s q r"),
+                                    dd_grouped[:], ALU.mult)
+        paired_a = gather_keys(2, "a", list_a)
+        turn_keys(paired_b, keys1[:, P : 2 * P, :])
+        paired_b = gather_keys(2, "b", list_b)
+        turn_keys(paired_a, keys2[:, 0:P, :])
+        paired_a = gather_keys(3, "a", list_a)
+        turn_keys(paired_b, keys2[:, P : 2 * P, :])
+        paired_b = gather_keys(3, "b", list_b, cuts=(0, 320, I))
+        keys3_a = grouped_tile("keys3_a", P, tag="scaled_b3_1")
+        turn_keys(paired_a, keys3_a[:])
+        turn_keys(paired_b, keys3_b[:])
+        grads_mx = quantize("grads", grads, tag="scaled_a3_0")
+        keys0_mx = quantize("keys0", keys0, tag="scaled_b3_0")
+        keys1_mx = quantize("keys1", keys1, tag="paired_a3")
+        keys2_mx = quantize("keys2", keys2, tag="keys0")
+        keys3_a_mx = quantize("keys3_a", keys3_a)
+        first_acc = psum.tile([P, P], F32, name="first_acc", tag="bank_v")
+        multiply(first_acc[:], cut(keys0_mx, 0, P), cut(keys0_mx, P, 2 * P))
+        middle_acc = psum.tile([P, 2 * P], F32, name="middle_acc", tag="bank_e")
+        multiply(middle_acc[:, 0:P], cut(keys1_mx, 0, P), cut(keys1_mx, P, 2 * P))
+        multiply(middle_acc[:, P : 2 * P], cut(keys2_mx, 0, P), cut(keys2_mx, P, 2 * P))
+        keys3_b_mx = quantize("keys3_b", keys3_b)
+        last_acc = psum.tile([P, P], F32, name="last_acc", tag="bank_a")
+        multiply(last_acc[:], keys3_a_mx, keys3_b_mx)
+        finish(first_acc, 0, P)
+        finish(middle_acc, P, 3 * P, tag="keys3_b")
+        finish(last_acc, 3 * P, 4 * P)

from contextlib import ExitStack

import concourse.mybir as mybir
from concourse.masks import make_identity

D, E, T, I, Q = 512, 512, 1024, 512, 128
FLOPS = 2 * Q * I * (2 * D + E) + 2 * 2 * Q * I * D

F32 = mybir.dt.float32
BF16 = mybir.dt.bfloat16
I32 = mybir.dt.int32
U32 = mybir.dt.uint32
U16 = mybir.dt.uint16
U8 = mybir.dt.uint8
FP8X4 = mybir.dt.float8_e4m3fn_x4
ACT = mybir.ActivationFunctionType
ALU = mybir.AluOpType

P = 128
PACK = 4
PLANES = D // P


def tile_attend_gsynonyms_kernel(tc, query, keys_words, keys_scales, gout, vals_words, vals_scales, lse, delta, fs,
                                  keyrows, ksc, res, offs, offs2, offs3, out):
    nc = tc.nc
    with ExitStack() as ctx:
        keep = ctx.enter_context(tc.tile_pool(name="keep", bufs=1))
        psum = ctx.enter_context(tc.psum_pool(name="psum", bufs=1))

        def load_list(name, src):
            tile = keep.tile([P, I // 16], U16, name=name)
            nc.sync.dma_start(tile[:], src)
            return tile

        def load_scales(name, src):
            tile = keep.tile([P, T], U8, name=name)
            rows = src[0].bitcast(I32)
            for quad in range(4):
                queue = nc.sync if quad < 2 else nc.scalar
                queue.dma_start(tile[32 * quad : 32 * quad + 32, :].bitcast(I32),
                                  rows[4 * quad : 4 * quad + 4, :].unsqueeze(0).to_broadcast([8, 4, T // 4]))
            return tile

        def load_words(name, src):
            tile = keep.tile([P, T], U32, name=name)
            nc.sync.dma_start(tile[:].bitcast(I32), src[0].rearrange("p t b -> p (t b)").bitcast(I32))
            return tile

        def load(name, shape, src):
            tile = keep.tile(shape, F32, name=name)
            nc.sync.dma_start(tile[:], src)
            return tile

        list_a = load_list("list_a", offs)
        key_scale_pool = load_scales("key_scale_pool", keys_scales)
        list_b = load_list("list_b", offs2)
        val_word_pool = load_words("val_word_pool", vals_words)
        list_v = load_list("list_v", offs3)
        val_scale_pool = load_scales("val_scale_pool", vals_scales)
        key_word_pool = load_words("key_word_pool", keys_words)
        gout_raw = load("gout_raw", [P, PACK, Q], gout.rearrange("(p r) q -> p r q", r=PACK))
        query_raw = load("query_raw", [P, PACK, Q], query.rearrange("(p r) q -> p r q", r=PACK))
        ksc_cols = load("ksc_cols", [P, PACK], ksc.rearrange("(s r) o -> s (r o)", r=PACK))
        key_planes = [load("key_plane0", [P, T], keyrows[0:P, :])]
        delta_col = load("delta_col", [P, 1], delta)
        lse_col = load("lse_col", [P, 1], lse)
        fs_cols = load("fs_cols", [P, PACK], fs.rearrange("o (s r) -> s (o r)", r=PACK))
        for j in range(1, PLANES):
            key_planes.append(load("key_plane%d" % j, [P, T], keyrows[j * P : (j + 1) * P, :]))
        res_rows = load("res_rows", [P, D], res)

        ident = keep.tile([P, P], F32, name="ident")
        make_identity(nc, ident[:])

        def gather(name, pool_tile, slots, dtype):
            tile = keep.tile([P, I], dtype, name=name, align_bytes=64)
            nc.vector.tensor_copy(tile[:], pool_tile[:].indirect(slots[:]))
            return tile

        def quantize(name, grouped, tag=""):
            width = grouped.shape[1]
            codes = keep.tile([P, width], U32, name=name + "_codes", tag=tag, align_bytes=64)
            scales = keep.tile([P, width], U8, name=name + "_scales", align_bytes=64)
            nc.vector.quantize_mx(codes[:].bitcast(FP8X4), scales[:], grouped[:].rearrange("p c r -> p (c r)"))
            return codes, scales

        def product(acc, stationary, moving, start, stop):
            nc.tensor.matmul_mx(acc, lhsT=stationary[0][:].bitcast(FP8X4), lhsT_scale=stationary[1][:],
                                rhs=moving[0][:].bitcast(FP8X4), rhs_scale=moving[1][:], start=start, stop=stop)

        def group_rows(name, raw):
            grouped = keep.tile([P, Q, PACK], BF16, name=name, align_bytes=64)
            nc.scalar.copy(grouped[:], raw[:].rearrange("p r q -> p q r"))
            return grouped

        def turn(name, bank, by_place):
            turned = psum.tile([P, PACK, Q], F32, name=name, tag=bank)
            for r in range(PACK):
                nc.tensor.transpose(turned[:, r, :], by_place[:, r, :], ident[:])
            return turned

        a_scales = gather("a_scales", key_scale_pool, list_a, U8)
        b_scales = gather("b_scales", key_scale_pool, list_b, U8)
        v_words = gather("v_words", val_word_pool, list_v, U32)
        v_scales = gather("v_scales", val_scale_pool, list_v, U8)
        gout_mx = quantize("gout", group_rows("gout_grouped", gout_raw))
        a_words = gather("a_words", key_word_pool, list_a, U32)
        query_mx = quantize("query", group_rows("query_grouped", query_raw))
        b_words = gather("b_words", key_word_pool, list_b, U32)

        ksc_turned = psum.tile([P, PACK, P], F32, name="ksc_turned", tag="bank_e")
        for r in range(PACK):
            nc.tensor.transpose(ksc_turned[:, r, :], ksc_cols[:, r : r + 1].to_broadcast([P, P]), ident[:])
        ksc_row = keep.tile([P, I], F32, name="ksc_row")
        nc.scalar.copy(ksc_row[:].rearrange("p (s r) -> p s r", r=PACK), ksc_turned[:].rearrange("p r s -> p s r"))

        neg_delta = keep.tile([P, 1], F32, name="neg_delta")
        nc.scalar.mul(neg_delta[:], delta_col[:], -1.0)
        neg_lse = keep.tile([P, 1], F32, name="neg_lse")
        nc.scalar.mul(neg_lse[:], lse_col[:], -1.0)

        def scores(name, bank, rows_mx, words, scales, func, bias):
            acc = psum.tile([P, I], F32, name=name + "_acc", tag=bank)
            product(acc[:], rows_mx, (words, scales), True, True)
            by_place = keep.tile([P, PACK, P], F32, name=name + "_by_place")
            nc.scalar.activation(by_place[:], acc[:].rearrange("q (s r) -> q r s", r=PACK), func, bias=bias[:])
            return by_place

        centred = scores("dp", "bank_v", gout_mx, v_words, v_scales, ACT.Identity, neg_delta)
        centred_t = turn("centred_t", "bank_e", centred)
        dd_by_place = keep.tile([P, PACK, Q], F32, name="dd_by_place")
        for r in range(PACK):
            nc.scalar.activation(dd_by_place[:, r, :], centred_t[:, r, :], ACT.Copy, scale=fs_cols[:, r : r + 1])
        dd_grouped = keep.tile([P, Q, PACK], F32, name="dd_grouped")
        nc.scalar.copy(dd_grouped[:], dd_by_place[:].rearrange("s r q -> s q r"))

        weights_t = []
        for name, words, scales in (("a", a_words, a_scales), ("b", b_words, b_scales)):
            weight = scores(name, "bank_" + name, query_mx, words, scales, ACT.Exp, neg_lse)
            weights_t.append(turn(name + "_weight_t", "bank_" + name, weight))

        def gather_keys(j, name, slots, cuts=(0, I)):
            paired = keep.tile([P, 2, P, 2], BF16, name="paired", tag="paired_%s%d" % (name, j), align_bytes=64)
            for piece in range(len(cuts) - 1):
                lo, hi = cuts[piece], cuts[piece + 1]
                scaled = keep.tile([P, hi - lo], F32, name="scaled", tag="scaled_%s%d_%d" % (name, j, piece), align_bytes=64)
                nc.vector.tensor_tensor(scaled[:], key_planes[j][:].indirect(slots[:, lo // 16 : hi // 16]),
                                        ksc_row[:, lo:hi], ALU.mult)
                nc.scalar.copy(paired[:, :, lo // PACK : hi // PACK, :],
                               scaled[:].rearrange("d (s u e) -> d u s e", u=2, e=2))
            return paired

        def turn_keys(paired, grouped):
            words = paired[:].rearrange("d u s e -> d (u s e)").bitcast(F32)
            turned = psum.tile([P, 2, P], F32, name="keys_turned", bufs=4)
            for u in range(2):
                nc.tensor.transpose(turned[:, u, :], words[:, u * P : (u + 1) * P], ident[:])
            nc.scalar.copy(grouped.rearrange("s d r -> s (d r)").bitcast(F32).rearrange("s (d u) -> s d u", u=2),
                           turned[:].rearrange("s u d -> s d u"))

        def cut(mx, lo, hi):
            return mx[0][:, lo:hi], mx[1][:, lo:hi]

        def multiply(acc, keys_a, keys_b):
            product(acc, cut(grads_mx, 0, Q), keys_a, True, False)
            product(acc, cut(grads_mx, Q, 2 * Q), keys_b, False, True)

        def finish(acc, lo, hi, tag=""):
            result = keep.tile([P, hi - lo], F32, name="result%d" % lo, tag=tag, align_bytes=64)
            nc.vector.tensor_tensor(result[:], acc[:], res_rows[:, lo:hi], ALU.add)
            nc.sync.dma_start(out[:, lo:hi], result[:])

        def grouped_tile(name, width, tag=""):
            return keep.tile([P, width, PACK], BF16, name=name, tag=tag or name, align_bytes=64)

        keys0 = grouped_tile("keys0", 2 * P)
        keys1 = grouped_tile("keys1", 2 * P)
        keys2 = grouped_tile("keys2", 2 * P)
        keys3_b = grouped_tile("keys3_b", P)

        paired_a = gather_keys(0, "a", list_a)
        paired_b = gather_keys(0, "b", list_b)
        turn_keys(paired_a, keys0[:, 0:P, :])
        paired_a = gather_keys(1, "a", list_a)
        turn_keys(paired_b, keys0[:, P : 2 * P, :])
        paired_b = gather_keys(1, "b", list_b)
        turn_keys(paired_a, keys1[:, 0:P, :])
        grads = grouped_tile("grads", 2 * Q)
        for side in range(2):
            nc.vector.tensor_tensor(grads[:, side * Q : (side + 1) * Q, :], weights_t[side][:].rearrange("s r q -> s q r"),
                                    dd_grouped[:], ALU.mult)
        paired_a = gather_keys(2, "a", list_a)
        turn_keys(paired_b, keys1[:, P : 2 * P, :])
        paired_b = gather_keys(2, "b", list_b)
        turn_keys(paired_a, keys2[:, 0:P, :])
        paired_a = gather_keys(3, "a", list_a)
        turn_keys(paired_b, keys2[:, P : 2 * P, :])
        paired_b = gather_keys(3, "b", list_b, cuts=(0, 320, I))
        keys3_a = grouped_tile("keys3_a", P, tag="scaled_b3_1")
        turn_keys(paired_a, keys3_a[:])
        turn_keys(paired_b, keys3_b[:])
        grads_mx = quantize("grads", grads, tag="scaled_a3_0")
        keys0_mx = quantize("keys0", keys0, tag="scaled_b3_0")
        keys1_mx = quantize("keys1", keys1, tag="paired_a3")
        keys2_mx = quantize("keys2", keys2, tag="keys0")
        keys3_a_mx = quantize("keys3_a", keys3_a)
        first_acc = psum.tile([P, P], F32, name="first_acc", tag="bank_v")
        multiply(first_acc[:], cut(keys0_mx, 0, P), cut(keys0_mx, P, 2 * P))
        middle_acc = psum.tile([P, 2 * P], F32, name="middle_acc", tag="bank_e")
        multiply(middle_acc[:, 0:P], cut(keys1_mx, 0, P), cut(keys1_mx, P, 2 * P))
        multiply(middle_acc[:, P : 2 * P], cut(keys2_mx, 0, P), cut(keys2_mx, P, 2 * P))
        keys3_b_mx = quantize("keys3_b", keys3_b)
        last_acc = psum.tile([P, P], F32, name="last_acc", tag="bank_a")
        multiply(last_acc[:], keys3_a_mx, keys3_b_mx)
        finish(first_acc, 0, P)
        finish(middle_acc, P, 3 * P, tag="keys3_b")
        finish(last_acc, 3 * P, 4 * P)
